import numpy as np
CORES = [6,14,22,30,38,134,142,150,158]
N = 9
T, EL, CAP, CAPP = 1024, 2, 480, 256
E = N * EL
def entries(a): return a.T.reshape(-1)
def pack(v, P): return np.ascontiguousarray(np.asarray(v, np.int32).reshape(-1, P).T)
def lists(rng, how):
    if how == "uniform": return {"ex": np.stack([pack(rng.permutation(np.repeat(np.arange(E), CAPP))[:T], 16) for r in range(N)])}
    R = np.arange(N)[:, None]; c = rng.permutation(E); C = np.zeros((N, E), np.int64)
    if how == "bands":
        a = c % N; C = CAPP * ((R >= a) & (R <= a + CAP // CAPP)); C[a, np.arange(E)] = np.where(c < N, CAPP, rng.integers(1, CAPP + 1, E))
    if how == "full":
        g = T // CAPP; C[:, c[:g]] = CAPP; C[:, c[:g // 2]] = rng.integers(CAPP // 2, CAPP + 1, (N, g // 2))
    if how in ("skew", "sorted"):
        V = np.full((N, 3), CAP // N); V[:, 0] = rng.integers(2, CAP // N + 1, N); h = rng.integers(1, N - 2); V[h, 0] = 0; V[h + 1, 0] = 1; V[rng.integers(N), 1:] += CAP % N; V[rng.integers(N), 2] += 1
        W = rng.random((N, E)) ** 4 + 1e-9; W[:, c[:3]] = 0
        C = np.minimum(((T - T // 8 - V.sum(axis=1, keepdims=True)) * W / W.sum(axis=1, keepdims=True)).astype(np.int64), CAPP); C[:, c[:3]] = V
    if how == "thin":
        C = rng.integers(0, CAP // N + 1, (N, E)); C[1] = 1; C[[0, N // 2, N - 1]] = 0
    X = np.stack([rng.permutation(np.concatenate([np.repeat(np.arange(E), C[r]), np.full(T - C[r].sum(), -1)])) for r in range(N)])
    if how == "sorted": X = np.sort(X, axis=1); X[1::2] = X[1::2, ::-1].copy()
    return {"ex": np.stack([pack(v, 16) for v in X])}
def blank(d):
    for r in range(0, N, 2):
        u, i = np.unique(entries(d["ex"][r])[::-1], return_index=True); d["x"][r][:, T - 1 - i[u >= 0]] = 0
def setup_inputs(rng):
    return dict({"x": rng.standard_normal((N, 128, T), dtype=np.float32)}, **lists(rng, "uniform"))
def setup_inputs_bands(rng):
    d = setup_inputs(rng); d.update(lists(rng, "bands"))
    for k in ("x",): d[k] = (d[k].astype(np.float32) * 1048576.0).astype(d[k].dtype)
    blank(d)
    return d
def setup_inputs_full(rng):
    d = setup_inputs(rng); d.update(lists(rng, "full"))
    for k in ("x",): d[k] = (d[k].astype(np.float32) * (1 / 1024.0)).astype(d[k].dtype)
    blank(d)
    return d
def setup_inputs_skew(rng):
    d = setup_inputs(rng); d.update(lists(rng, "skew"))
    blank(d)
    return d
def setup_inputs_sorted(rng):
    d = setup_inputs(rng); d.update(lists(rng, "sorted"))
    blank(d)
    return d
def setup_inputs_thin(rng):
    d = setup_inputs(rng); d.update(lists(rng, "thin"))
    blank(d)
    return d
def check_inputs(x):
    bad = []
    if x["ex"].min() < -1 or x["ex"].max() >= E: bad.append("ex out of range")
    if max(int(np.bincount(entries(a)[entries(a) >= 0], minlength=E).max()) for a in x["ex"]) > CAPP: bad.append("more than CAPP tokens of one rank choose one expert")
    return bad
def reference(x, ex):
    X = np.concatenate(list(x), axis=1); e = np.concatenate([entries(a) for a in ex])
    k = np.nonzero(e >= 0)[0]; o = k[np.argsort(e[k], kind="stable")]; s = e[o]
    p = np.arange(len(o)) - np.searchsorted(s, s)
    Y = np.zeros((128, E * CAP), x.dtype); m = p < CAP; Y[:, CAP * s[m] + p[m]] = X[:, o[m]]
    return {"y": np.stack([Y[:, EL * CAP * r:EL * CAP * (r + 1)] for r in range(N)])}

@@ -1,0 +1,345 @@
+from concourse.bass import DstId, RemoteDMATransfer
+from concourse.mybir import AluOpType as Op, AxisListType, ActivationFunctionType as Act
+
+N, T_, EL, CAP, CAPP = 9, 1024, 2, 480, 256
+E = N * EL
+W = EL * CAPP
+ZERO = N * W
+NC = 8
+KC = NC * E
+BIG = 8192.0
+MAXB = 5 * 32
+LW = CAP // 16
+
+PLAN = [[2, 4, 6, 8], [1, 3, 5, 7]]
+
+SCRATCH = {
+    "xs": ("sbuf", [128, T_], "float32"),
+    "exsb": ("sbuf", [128, NC], "int32"),
+    "exall": ("dram", [N * 128, NC], "int32"),
+    "exs": ("sbuf", [128, 128], "int32"),
+    "land": ("sbuf", [128, N * W + 16], "float32"),
+    "pk": ("sbuf", [128, 4 * W], "float32"),
+    "yt": ("sbuf", [128, EL * CAP], "float32"),
+    "pcol": ("sbuf", [128, 1], "int32"),
+    "frow": ("sbuf", [128, 128], "int32"),
+    "kio": ("sbuf", [128, KC], "int32"),
+    "krow": ("sbuf", [128, 128], "int32"),
+    "hrow": ("sbuf", [128, 128], "int32"),
+    "lcoli": ("sbuf", [128, 1], "int32"),
+    "hcoli": ("sbuf", [128, 1], "int32"),
+    "icoli": ("sbuf", [128, 1], "int32"),
+    "lcol": ("sbuf", [128, 1], "float32"),
+    "hcol": ("sbuf", [128, 1], "float32"),
+    "icol": ("sbuf", [128, 1], "float32"),
+    "pcolf": ("sbuf", [128, 1], "float32"),
+    "kcol": ("sbuf", [128, 1], "float32"),
+    "otf": ("sbuf", [128, NC + 1], "float32"),
+    "oti": ("sbuf", [128, NC + 1], "int32"),
+    "offe": ("sbuf", [128, 16], "uint16"),
+    "mlt": ("sbuf", [128, 128], "bfloat16"),
+    "mle": ("sbuf", [128, 128], "bfloat16"),
+    "mdg": ("sbuf", [128, 128], "bfloat16"),
+    "bigi": ("sbuf", [128, 128], "bfloat16"),
+    "ones": ("sbuf", [128, 128], "bfloat16"),
+    "k256": ("sbuf", [128, KC], "bfloat16"),
+    "resetm": ("sbuf", [128, KC], "float32"),
+    "oh": ("sbuf", [128, KC], "bfloat16"),
+    "rr": ("sbuf", [128, KC], "float32"),
+    "jcol": ("sbuf", [128, NC], "float32"),
+    "mrowi": ("sbuf", [128, 128], "int32"),
+    "mrow": ("sbuf", [128, 128], "float16"),
+    "bio": ("sbuf", [128, MAXB], "float16"),
+    "hii": ("sbuf", [128, NC], "int32"),
+    "hif": ("sbuf", [128, NC], "float32"),
+    "h16": ("sbuf", [128, NC], "float32"),
+    "lo": ("sbuf", [128, NC], "float32"),
+    "at": ("sbuf", [128, NC * 128], "float16"),
+    "bt": ("sbuf", [128, NC * MAXB], "float16"),
+    "offu": ("sbuf", [128, MAXB], "uint16"),
+    "ident": ("sbuf", [128, 128], "float16"),
+    "pl": ("sbuf", [128, LW], "float16"),
+    "plb": ("sbuf", [128, EL * LW], "float16"),
+    "rmask": ("sbuf", [128, 10], "bfloat16"),
+    "eqt": ("sbuf", [128, EL * 128], "float32"),
+    "cnt": ("sbuf", [128, EL], "float32"),
+    "prhs": ("sbuf", [128, EL * 10], "bfloat16"),
+    "pst": ("sbuf", [128, EL * 10], "float32"),
+    "pdf": ("sbuf", [128, EL * 10], "float32"),
+    "jmp": ("sbuf", [128, EL * 10], "float32"),
+    "tt": ("sbuf", [128, N * EL * LW], "float16"),
+    "offy": ("sbuf", [128, EL * LW], "uint16"),
+    "psc": ("psum", [128, 512], "float32"),
+    "pso": ("psum", [128, 512], "float32"),
+    "psp": ("psum", [128, 512], "float32"),
+    "psi": ("psum", [128, 512], "float32"),
+}
+SEMAPHORES = ["gi", "vs", "ss", "pe", "ldex", "ldexd", "ldx0", "ldx1", "ldexs", "sty0", "sty1",
+              "hex", "hx0", "hx1", "exarr", "arr", "ls"]
+
+
+def _bits(m):
+    return bin(m).count("1")
+
+
+def _team(rank, T, topo):
+    me = T.cores[rank]
+    same = [c for c in range(256) if topo.host(c) == topo.host(me) and topo.chip(c) == topo.chip(me)
+            and c not in T.cores and all(topo.may_write(c, d) for d in T.cores)]
+    same.sort(key=lambda c: (topo.die(c) == topo.die(me), c))
+    return ([me] + same)[:len(PLAN)]
+
+
+def rank_program(g, core, T, topo):
+    rank, seat = None, None
+    for r in range(N):
+        team = _team(r, T, topo)
+        if core in team:
+            rank, seat = r, team.index(core)
+            break
+    if rank is None:
+        return
+    main = seat == 0
+    team = _team(rank, T, topo)
+    dests = [(rank + s) % N for s in PLAN[seat]]
+    blocks = dests + ([rank] if main else [])
+    nb = 32 * len(blocks)
+    S = T.sem
+    n = {"v": 0, "s": 0, "p": 0, "g": 0, "ls": 0}
+    eng = {"v": g.vector, "s": g.scalar, "p": g.tensor, "g": g, "y": g.sync}
+    semof = {"v": S.vs, "s": S.ss, "p": S.pe, "g": S.gi}
+    seen = {}
+
+    def need(q, name, sem, val):
+        if val > 0 and seen.get((q, name), 0) < val:
+            eng[q].wait_ge(sem, val)
+            seen[(q, name)] = val
+
+    def after(q, **k):
+        for name, val in k.items():
+            need(q, name, semof[name], val)
+
+    def done(q, ins):
+        ins.then_inc(semof[q], 1)
+        n[q] += 1
+        return n[q]
+
+    V, PE, SC = g.vector, g.tensor, g.scalar
+
+    if main:
+        g.sync.dma_start(T.exsb[:], T.ex[:]).then_inc(S.ldex, 16)
+        g.scalar.dma_start(T.exall[rank * 128:(rank + 1) * 128, :], T.ex[:]).then_inc(S.ldexd, 16)
+        g.sync.dma_start(T.xs[:, 0:512], T.x[:, 0:512]).then_inc(S.ldx0, 16)
+        g.scalar.dma_start(T.xs[:, 512:1024], T.x[:, 512:1024]).then_inc(S.ldx1, 16)
+    hm = [0] * len(team)
+    if len(team) > 1:
+        off = 0
+        for d in T.cores:
+            if d != team[0]:
+                off |= topo.mask(team[0], d)
+        for i in range(1, len(team)):
+            hm[i] = topo.mask(team[0], team[i])
+        hx = hm[1] & ~off
+
+    done("g", g.iota(T.pcol[:], [[0, 1]], 0, 1))
+    done("g", g.iota(T.frow[:], [[1, 128]], 0, 0))
+    done("g", g.iota(T.kio[:], [[0, NC], [1, E]], 0, 0))
+    done("g", g.iota(T.hrow[:], [[0, 16], [1, 8]], 0, 0))
+    done("g", g.iota(T.krow[:], [[1, 16], [128, 8]], 0, 0))
+
+    if main:
+        need("g", "ldexd", S.ldexd, 16)
+        src = T.exall[rank * 128:(rank + 1) * 128, :]
+        ids, dst, mask = [], [], 0xFFFFFFFF
+        for s in [s for p in PLAN for s in p]:
+            d = T.cores[(rank + s) % N]
+            rid, pid = topo.addr(d, core)
+            ids.append(DstId(rid=rid, pnc=pid))
+            dst.append(T.exall[rank * 128:(rank + 1) * 128, :])
+            mask &= topo.mask(core, d)
+        tr = []
+        for i in range(1, len(team)):
+            rid, pid = topo.addr(team[i], core)
+            m = hx
+            tr.append(RemoteDMATransfer(dst_ids=[DstId(rid=rid, pnc=pid)], dma_engine_mask=m, remote_sem=S.hex,
+                                        srcs=[src], dsts=[T.exsb[:]]))
+            n["ls"] += _bits(m)
+        tr.append(RemoteDMATransfer(dst_ids=ids, dma_engine_mask=mask, remote_sem=S.exarr, srcs=[src], dsts=dst))
+        n["ls"] += _bits(mask)
+        g.remote_dma_fused(tr, local_sem=S.ls)
+        for h, (ld, hs) in enumerate(((S.ldx0, S.hx0), (S.ldx1, S.hx1))):
+            need("g", "ldx%d" % h, ld, 16)
+            for i in range(1, len(team)):
+                rid, pid = topo.addr(team[i], core)
+                sl = T.xs[:, 512 * h:512 * (h + 1)]
+                g.remote_dma(sl, sl, hs, S.ls, pid, rid, hm[i])
+                n["ls"] += _bits(hm[i])
+
+    after("v", g=1)
+    a = done("v", V.tensor_scalar(T.lcoli[:], T.pcol[:], 15, None, Op.bitwise_and))
+    done("v", V.tensor_scalar(T.hcoli[:], T.pcol[:], 7, None, Op.bitwise_and))
+    a = done("v", V.tensor_scalar(T.icoli[:], T.pcol[:], 3, None, Op.arith_shift_right))
+    done("v", V.memset(T.ones[:], 1.0))
+    if main:
+        done("v", V.memset(T.land[:, ZERO:ZERO + 16], 0.0))
+    after("v", v=a)
+    done("v", V.tensor_copy(T.lcol[:], T.lcoli[:]))
+    done("v", V.tensor_copy(T.hcol[:], T.hcoli[:]))
+    done("v", V.tensor_copy(T.icol[:], T.icoli[:]))
+    a = done("v", V.tensor_copy(T.pcolf[:], T.pcol[:]))
+    after("v", v=a, g=2)
+    b = done("v", V.tensor_scalar(T.otf[:], T.frow[:, 0:NC + 1], 16.0, T.lcol[:], Op.mult, Op.add))
+    done("v", V.tensor_scalar(T.bigi[:], T.frow[:], T.pcolf[:], BIG, Op.is_equal, Op.mult))
+    a = done("v", V.tensor_scalar(T.kcol[:], T.hcoli[:], 128.0, T.icol[:], Op.mult, Op.add))
+    after("v", v=b)
+    b = done("v", V.tensor_scalar(T.oti[:], T.otf[:], -8.5, 1.0 / E, Op.add, Op.mult))
+    after("v", g=5)
+    done("v", V.tensor_scalar(T.mlt[:], T.hrow[:], T.hcol[:], None, Op.is_gt))
+    done("v", V.tensor_scalar(T.mle[:], T.hrow[:], T.hcol[:], None, Op.is_ge))
+    after("v", v=b)
+    b = done("v", V.tensor_copy(T.offe[:, 0:NC + 1], T.oti[:]))
+    done("v", V.tensor_scalar(T.mdg[:], T.krow[:], T.kcol[:], None, Op.is_gt))
+    kdone = done("v", V.tensor_scalar(T.k256[0:1, :], T.kio[0:1, :], float(CAPP), None, Op.mult))
+    after("v", v=b)
+    if main:
+        need("v", "ldex", S.ldex, 16)
+    else:
+        need("v", "hex", S.hex, _bits(hx))
+    ohd = done("v", V.tensor_tensor(T.oh[:], T.exsb[:, 0:NC].indirect(T.offe[:, 0:NC + 1]), T.kio[:], Op.is_equal))
+    rsd = done("v", V.tensor_scalar(T.resetm[:], T.kio[:], 0, None, Op.is_gt))
+    done("v", V.tensor_scalar(T.jcol[:], T.frow[:, 0:NC], 16.0, T.kcol[:], Op.mult, Op.add))
+    b = done("v", V.tensor_scalar(T.mrowi[:], T.frow[:], 15, None, Op.bitwise_and))
+    for q, d in enumerate(blocks):
+        done("v", V.tensor_scalar(T.bio[:, 32 * q:32 * q + 32], T.frow[:, 0:32], 32.0 * d, None, Op.add))
+    after("v", v=b)
+    cd = done("v", V.tensor_copy(T.mrow[:], T.mrowi[:]))
+
+    after("p", v=kdone)
+    ps = T.psc
+    PE.matmul(ps[:, 0:KC], T.ones[0:1, :], T.k256[0:1, :], True, False)
+    after("p", v=ohd)
+    PE.matmul(ps[:, 0:KC], T.mdg[:], T.oh[:], False, False)
+    for d in range(1, NC):
+        PE.matmul(ps[:, E * d:KC], T.mle[:], T.oh[:, 0:KC - E * d], False, False)
+        PE.matmul(ps[:, 0:KC - E * d], T.mlt[:], T.oh[:, E * d:KC], False, False)
+    a = done("p", PE.matmul(ps[:, 0:KC], T.bigi[:], T.oh[:], False, True))
+
+    after("v", p=a, v=cd)
+    a = done("v", V.tensor_tensor_scan(T.rr[:], T.resetm[:], ps[:, 0:KC], 0.0, Op.mult, Op.max))
+    after("v", v=a)
+    sl = T.rr[:, E - 1::E]
+    a = done("v", V.tensor_scalar(T.hii[:], sl, -(BIG + 7.5), 1.0 / 16, Op.add, Op.mult))
+    after("v", v=a)
+    done("v", V.tensor_copy(T.hif[:], T.hii[:]))
+    a = done("v", V.tensor_scalar(T.h16[:], T.hii[:], -16.0, -BIG, Op.mult, Op.add))
+    after("v", v=a)
+    a = done("v", V.tensor_tensor(T.lo[:], T.h16[:], sl, Op.add))
+    bds = []
+    for c in range(NC):
+        if c == 1:
+            after("v", v=a)
+        done("v", V.tensor_scalar(T.bt[:, nb * c:nb * (c + 1)], T.bio[:, 0:nb], T.hif[:, c:c + 1], None, Op.is_equal))
+        if c == 0:
+            after("v", v=a)
+        bds.append(done("v", V.tensor_scalar(T.at[:, 128 * c:128 * (c + 1)], T.mrow[:], T.lo[:, c:c + 1],
+                                             T.jcol[:, c:c + 1], Op.is_equal, Op.mult)))
+    for c in range(NC):
+        after("p", v=bds[c])
+        ins = PE.matmul(T.pso[:, 0:nb], T.at[:, 128 * c:128 * (c + 1)], T.bt[:, nb * c:nb * (c + 1)], c == 0, c == NC - 1)
+    a = done("p", ins)
+    after("v", p=a)
+    offd = done("v", V.tensor_copy(T.offu[:, 0:nb], T.pso[:, 0:nb]))
+
+    for q in ("v", "s"):
+        after(q, v=offd)
+        if main:
+            need(q, "ldx0", S.ldx0, 16)
+            need(q, "ldx1", S.ldx1, 16)
+        else:
+            need(q, "hx0", S.hx0, _bits(hm[seat]))
+            need(q, "hx1", S.hx1, _bits(hm[seat]))
+    for q, d in enumerate(blocks):
+        if d == rank:
+            o0 = T.land[:, rank * W:rank * W + CAPP]
+            o1 = T.land[:, rank * W + CAPP:(rank + 1) * W]
+        else:
+            o0 = T.pk[:, q * W:q * W + CAPP]
+            o1 = T.pk[:, q * W + CAPP:(q + 1) * W]
+        va = done("v", V.tensor_copy(o0, T.xs[:].indirect(T.offu[:, 32 * q:32 * q + 16])))
+        sa = done("s", SC.activation(o1, T.xs[:].indirect(T.offu[:, 32 * q + 16:32 * q + 32]), Act.Copy))
+        if d != rank:
+            after("g", v=va, s=sa)
+            rid, pid = topo.addr(T.cores[d], core)
+            m = topo.mask(core, T.cores[d])
+            g.remote_dma(T.land[:, rank * W:(rank + 1) * W], T.pk[:, q * W:(q + 1) * W], S.arr, S.ls, pid, rid, m)
+            n["ls"] += _bits(m)
+
+    if main:
+        done("v", V.tensor_scalar(T.ident[:], T.frow[:], T.pcolf[:], None, Op.is_equal))
+        b = done("v", V.tensor_scalar(T.pl[:], T.frow[:, 0:LW], 16.0, T.lcol[:], Op.mult, Op.add))
+        done("v", V.tensor_scalar(T.rmask[0:8 * N, :], T.frow[0:8 * N, 0:10], T.icol[0:8 * N, :], None, Op.is_gt))
+        after("v", v=b)
+        for e in range(EL):
+            done("v", V.tensor_scalar(T.plb[:, e * LW:(e + 1) * LW], T.pl[:], float(e * CAPP), None, Op.add))
+        total = 0
+        exn = 0
+        for r in range(N):
+            if r != rank:
+                mm = 0xFFFFFFFF
+                for d in T.cores:
+                    if d != T.cores[r]:
+                        mm &= topo.mask(T.cores[r], d)
+                exn += _bits(mm)
+                tm = _team(r, T, topo)
+                for i, p in enumerate(PLAN):
+                    for s in p:
+                        if (r + s) % N == rank:
+                            total += _bits(topo.mask(tm[i], core))
+        need("y", "ldexd", S.ldexd, 16)
+        need("y", "exarr", S.exarr, exn)
+        g.sync.dma_start(T.exs[0:8 * N, :], T.exall[:]).then_inc(S.ldexs, 16)
+        need("v", "ldexs", S.ldexs, 16)
+        for e in range(EL):
+            b = done("v", V.tensor_scalar(T.eqt[0:8 * N, 128 * e:128 * e + 128], T.exs[0:8 * N, :], EL * rank + e, None,
+                                          Op.is_equal))
+        after("v", v=b)
+        for e in range(EL):
+            b = done("v", V.tensor_reduce(T.cnt[0:8 * N, e:e + 1], T.eqt[0:8 * N, 128 * e:128 * e + 128], AxisListType.X, Op.add))
+        after("v", v=b)
+        for e in range(EL):
+            b = done("v", V.tensor_scalar(T.prhs[0:8 * N, 10 * e:10 * e + 10], T.rmask[0:8 * N, :], T.cnt[0:8 * N, e:e + 1],
+                                          None, Op.mult))
+        after("p", v=b)
+        a = done("p", PE.matmul(T.psp[:, 0:EL * 10], T.ones[0:8 * N, :], T.prhs[0:8 * N, :], True, True))
+        after("v", p=a)
+        b = done("v", V.tensor_copy(T.pst[:], T.psp[:, 0:EL * 10]))
+        after("v", v=b)
+        b = done("v", V.tensor_tensor(T.pdf[:, 0:EL * 10 - 1], T.pst[:, 1:EL * 10], T.pst[:, 0:EL * 10 - 1], Op.subtract))
+        after("v", v=b)
+        b = done("v", V.tensor_scalar(T.jmp[:, 0:EL * 10 - 1], T.pdf[:, 0:EL * 10 - 1], -1.0, float(W), Op.mult, Op.add))
+        after("v", v=b)
+        PE.matmul(T.psi[:, 0:EL * LW], T.ident[:], T.plb[:], True, False)
+        for r in range(1, N + 1):
+            for e in range(EL):
+                o = T.tt[:, (r - 1) * EL * LW + e * LW:(r - 1) * EL * LW + (e + 1) * LW]
+                j = T.jmp[:, 10 * e + r - 1:10 * e + r] if r < N else BIG
+                b = done("v", V.tensor_scalar(o, T.pl[:], T.pst[:, 10 * e + r:10 * e + r + 1], j, Op.is_ge, Op.mult))
+            after("p", v=b)
+            ins = PE.matmul(T.psi[:, 0:EL * LW], T.ident[:], T.tt[:, (r - 1) * EL * LW:r * EL * LW], False, r == N)
+        a = done("p", ins)
+        after("v", p=a)
+        b = done("v", V.tensor_scalar(T.offy[:], T.psi[:, 0:EL * LW], float(ZERO), None, Op.min))
+        after("v", v=b, s=n["s"])
+        after("s", v=b, s=n["s"])
+        need("v", "arr", S.arr, total)
+        need("s", "arr", S.arr, total)
+        a = done("v", V.tensor_copy(T.yt[:, 0:CAP], T.land[:].indirect(T.offy[:, 0:LW])))
+        b = done("s", SC.activation(T.yt[:, CAP:2 * CAP], T.land[:].indirect(T.offy[:, LW:2 * LW]), Act.Copy))
+        after("y", v=a)
+        g.sync.dma_start(T.y[:, 0:CAP], T.yt[:, 0:CAP]).then_inc(S.sty0, 16)
+        after("s", s=b)
+        g.scalar.dma_start(T.y[:, CAP:2 * CAP], T.yt[:, CAP:2 * CAP]).then_inc(S.sty1, 16)
+        need("g", "sty0", S.sty0, 16)
+        need("g", "sty1", S.sty1, 16)
+    after("g", v=n["v"], s=n["s"], p=n["p"], g=n["g"])
+    g.wait_ge(S.ls, n["ls"])

@@ -6,12 +6,16 @@ E = N * EL
 W = EL * CAPP
 ZERO = N * W
 NC = 8
-KC = NC * E
+KS = 8
+KC = NC * KS
 BIG = 8192.0
-MAXB = 5 * 32
 LW = CAP // 16
 
-PLAN = [[2, 4, 6, 8], [1, 3, 5, 7]]
+PLAN = [[(2, (0, 1)), (6, (0, 1)), (7, (0,))], [(1, (0, 1)), (5, (0, 1))], [(4, (0, 1)), (8, (0, 1))],
+        [(3, (0, 1)), (7, (1,))]]
+FEED = [None, 0, 0, 1]
+LISTS = [[], [1, 5], [2, 6, 8], [3, 7, 4]]
+NBMAX = 16 * 7
 
 SCRATCH = {
     "xs": ("sbuf", [128, T_], "float32"),
@@ -19,24 +23,18 @@ SCRATCH = {
     "exall": ("dram", [N * 128, NC], "int32"),
     "exs": ("sbuf", [128, 128], "int32"),
     "land": ("sbuf", [128, N * W + 16], "float32"),
-    "pk": ("sbuf", [128, 4 * W], "float32"),
+    "pk": ("sbuf", [128, 3 * W], "float32"),
     "yt": ("sbuf", [128, EL * CAP], "float32"),
-    "pcol": ("sbuf", [128, 1], "int32"),
-    "frow": ("sbuf", [128, 128], "int32"),
-    "kio": ("sbuf", [128, KC], "int32"),
-    "krow": ("sbuf", [128, 128], "int32"),
-    "hrow": ("sbuf", [128, 128], "int32"),
-    "lcoli": ("sbuf", [128, 1], "int32"),
-    "hcoli": ("sbuf", [128, 1], "int32"),
-    "icoli": ("sbuf", [128, 1], "int32"),
-    "lcol": ("sbuf", [128, 1], "float32"),
-    "hcol": ("sbuf", [128, 1], "float32"),
-    "icol": ("sbuf", [128, 1], "float32"),
-    "pcolf": ("sbuf", [128, 1], "float32"),
+    "ci": ("sbuf", [128, 8], "int32"),
+    "cf": ("sbuf", [128, 8], "float32"),
     "kcol": ("sbuf", [128, 1], "float32"),
-    "otf": ("sbuf", [128, NC + 1], "float32"),
-    "oti": ("sbuf", [128, NC + 1], "int32"),
-    "offe": ("sbuf", [128, 16], "uint16"),
+    "jb": ("sbuf", [128, 1], "float32"),
+    "kio": ("sbuf", [128, KC], "int32"),
+    "frow": ("sbuf", [128, 128], "bfloat16"),
+    "hrow": ("sbuf", [128, 128], "bfloat16"),
+    "krow": ("sbuf", [128, 128], "bfloat16"),
+    "mrow": ("sbuf", [128, 128], "bfloat16"),
+    "offe": ("sbuf", [128, 4], "uint16"),
     "mlt": ("sbuf", [128, 128], "bfloat16"),
     "mle": ("sbuf", [128, 128], "bfloat16"),
     "mdg": ("sbuf", [128, 128], "bfloat16"),
@@ -47,16 +45,13 @@ SCRATCH = {
     "oh": ("sbuf", [128, KC], "bfloat16"),
     "rr": ("sbuf", [128, KC], "float32"),
     "jcol": ("sbuf", [128, NC], "float32"),
-    "mrowi": ("sbuf", [128, 128], "int32"),
-    "mrow": ("sbuf", [128, 128], "float16"),
-    "bio": ("sbuf", [128, MAXB], "float16"),
     "hii": ("sbuf", [128, NC], "int32"),
     "hif": ("sbuf", [128, NC], "float32"),
     "h16": ("sbuf", [128, NC], "float32"),
     "lo": ("sbuf", [128, NC], "float32"),
     "at": ("sbuf", [128, NC * 128], "float16"),
-    "bt": ("sbuf", [128, NC * MAXB], "float16"),
-    "offu": ("sbuf", [128, MAXB], "uint16"),
+    "bt": ("sbuf", [128, NC * NBMAX], "float16"),
+    "offu": ("sbuf", [128, NBMAX], "uint16"),
     "ident": ("sbuf", [128, 128], "float16"),
     "pl": ("sbuf", [128, LW], "float16"),
     "plb": ("sbuf", [128, EL * LW], "float16"),
@@ -74,8 +69,7 @@ SCRATCH = {
     "psp": ("psum", [128, 512], "float32"),
     "psi": ("psum", [128, 512], "float32"),
 }
-SEMAPHORES = ["gi", "vs", "ss", "pe", "ldex", "ldexd", "ldx0", "ldx1", "ldexs", "sty0", "sty1",
-              "hex", "hx0", "hx1", "exarr", "arr", "ls"]
+SEMAPHORES = ["gi", "vs", "ss", "pe", "ldex", "ldexd", "ldx", "ldexs", "sty0", "sty1", "hex", "hx", "exarr", "arr", "ls"]
 
 
 def _bits(m):
@@ -85,39 +79,39 @@ def _bits(m):
 def _team(rank, T, topo):
     me = T.cores[rank]
     same = [c for c in range(256) if topo.host(c) == topo.host(me) and topo.chip(c) == topo.chip(me)
-            and c not in T.cores and all(topo.may_write(c, d) for d in T.cores)]
-    same.sort(key=lambda c: (topo.die(c) == topo.die(me), c))
-    return ([me] + same)[:len(PLAN)]
+            and c != me and all(topo.may_write(c, d) for d in T.cores)]
+    far = [c for c in same if topo.die(c) != topo.die(me)]
+    near = [c for c in same if topo.die(c) == topo.die(me)]
+    return [me, far[0], near[0], far[1]]
 
 
 def rank_program(g, core, T, topo):
-    rank, seat = None, None
+    teams = [_team(r, T, topo) for r in range(N)]
+    rank = None
     for r in range(N):
-        team = _team(r, T, topo)
-        if core in team:
-            rank, seat = r, team.index(core)
-            break
+        if core in teams[r]:
+            rank, seat = r, teams[r].index(core)
     if rank is None:
         return
+    team = teams[rank]
     main = seat == 0
-    team = _team(rank, T, topo)
-    dests = [(rank + s) % N for s in PLAN[seat]]
-    blocks = dests + ([rank] if main else [])
-    nb = 32 * len(blocks)
+    blocks = [((rank + s) % N, es) for s, es in PLAN[seat]] + ([(rank, (0, 1))] if main else [])
+    mine = [EL * d + e for d, es in blocks for e in es]
+    nb = 16 * len(mine)
     S = T.sem
     n = {"v": 0, "s": 0, "p": 0, "g": 0, "ls": 0}
     eng = {"v": g.vector, "s": g.scalar, "p": g.tensor, "g": g, "y": g.sync}
     semof = {"v": S.vs, "s": S.ss, "p": S.pe, "g": S.gi}
     seen = {}
 
-    def need(q, name, sem, val):
+    def need(q, name, val):
         if val > 0 and seen.get((q, name), 0) < val:
-            eng[q].wait_ge(sem, val)
+            eng[q].wait_ge(semof[name] if name in semof else S[name], val)
             seen[(q, name)] = val
 
     def after(q, **k):
         for name, val in k.items():
-            need(q, name, semof[name], val)
+            need(q, name, val)
 
     def done(q, ins):
         ins.then_inc(semof[q], 1)
@@ -129,90 +123,83 @@ def rank_program(g, core, T, topo):
     if main:
         g.sync.dma_start(T.exsb[:], T.ex[:]).then_inc(S.ldex, 16)
         g.scalar.dma_start(T.exall[rank * 128:(rank + 1) * 128, :], T.ex[:]).then_inc(S.ldexd, 16)
-        g.sync.dma_start(T.xs[:, 0:512], T.x[:, 0:512]).then_inc(S.ldx0, 16)
-        g.scalar.dma_start(T.xs[:, 512:1024], T.x[:, 512:1024]).then_inc(S.ldx1, 16)
-    hm = [0] * len(team)
-    if len(team) > 1:
-        off = 0
-        for d in T.cores:
-            if d != team[0]:
-                off |= topo.mask(team[0], d)
-        for i in range(1, len(team)):
-            hm[i] = topo.mask(team[0], team[i])
-        hx = hm[1] & ~off
+        g.sync.dma_start(T.xs[:], T.x[:]).then_inc(S.ldx, 16)
+    hx = topo.mask(team[0], team[1]) & topo.mask(team[0], team[2]) & topo.mask(team[0], team[3])
 
-    done("g", g.iota(T.pcol[:], [[0, 1]], 0, 1))
-    done("g", g.iota(T.frow[:], [[1, 128]], 0, 0))
-    done("g", g.iota(T.kio[:], [[0, NC], [1, E]], 0, 0))
-    done("g", g.iota(T.hrow[:], [[0, 16], [1, 8]], 0, 0))
-    done("g", g.iota(T.krow[:], [[1, 16], [128, 8]], 0, 0))
+    fl = {"allow_small_or_imprecise_dtypes": True}
+    done("g", g.iota(T.ci[:, 0:1], [[0, 1]], 0, 1))
+    done("g", g.iota(T.frow[:], [[1, 128]], 0, 0, **fl))
+    done("g", g.iota(T.krow[:], [[1, 16], [16, 8]], 0, 0, **fl))
+    done("g", g.iota(T.hrow[:], [[0, 16], [1, 8]], 0, 0, **fl))
 
+    slot = T.exall[rank * 128:(rank + 1) * 128, :]
     if main:
-        need("g", "ldexd", S.ldexd, 16)
-        src = T.exall[rank * 128:(rank + 1) * 128, :]
-        ids, dst, mask = [], [], 0xFFFFFFFF
-        for s in [s for p in PLAN for s in p]:
+        need("g", "ldexd", 16)
+        ids = []
+        for c in team[1:]:
+            rid, pid = topo.addr(c, core)
+            ids.append(DstId(rid=rid, pnc=pid))
+        g.remote_dma_fused([RemoteDMATransfer(dst_ids=ids, dma_engine_mask=hx, remote_sem=S.hex, srcs=[slot],
+                                              dsts=[T.exsb[:]] * len(ids))], local_sem=S.ls)
+        n["ls"] += _bits(hx)
+    done("g", g.iota(T.mrow[:], [[0, 8], [1, 16]], 0, 0, **fl))
+    if LISTS[seat]:
+        need("g", "hex", _bits(hx))
+        ids, mask = [], topo.mask(core, T.cores[(rank + LISTS[seat][0]) % N])
+        for s in LISTS[seat]:
             d = T.cores[(rank + s) % N]
             rid, pid = topo.addr(d, core)
             ids.append(DstId(rid=rid, pnc=pid))
-            dst.append(T.exall[rank * 128:(rank + 1) * 128, :])
             mask &= topo.mask(core, d)
-        tr = []
-        for i in range(1, len(team)):
-            rid, pid = topo.addr(team[i], core)
-            m = hx
-            tr.append(RemoteDMATransfer(dst_ids=[DstId(rid=rid, pnc=pid)], dma_engine_mask=m, remote_sem=S.hex,
-                                        srcs=[src], dsts=[T.exsb[:]]))
-            n["ls"] += _bits(m)
-        tr.append(RemoteDMATransfer(dst_ids=ids, dma_engine_mask=mask, remote_sem=S.exarr, srcs=[src], dsts=dst))
+        g.remote_dma_fused([RemoteDMATransfer(dst_ids=ids, dma_engine_mask=mask, remote_sem=S.exarr,
+                                              srcs=[T.exsb[:]], dsts=[slot] * len(ids))], local_sem=S.ls)
         n["ls"] += _bits(mask)
-        g.remote_dma_fused(tr, local_sem=S.ls)
-        for h, (ld, hs) in enumerate(((S.ldx0, S.hx0), (S.ldx1, S.hx1))):
-            need("g", "ldx%d" % h, ld, 16)
-            for i in range(1, len(team)):
-                rid, pid = topo.addr(team[i], core)
-                sl = T.xs[:, 512 * h:512 * (h + 1)]
-                g.remote_dma(sl, sl, hs, S.ls, pid, rid, hm[i])
-                n["ls"] += _bits(hm[i])
+    fed = [team[i] for i in range(len(team)) if FEED[i] == seat]
+    if fed:
+        if main:
+            need("g", "ldx", 16)
+        else:
+            need("g", "hx", _bits(hx))
+        ids = []
+        for c in fed:
+            rid, pid = topo.addr(c, core)
+            ids.append(DstId(rid=rid, pnc=pid))
+        g.remote_dma_fused([RemoteDMATransfer(dst_ids=ids, dma_engine_mask=hx, remote_sem=S.hx, srcs=[T.xs[:]],
+                                              dsts=[T.xs[:]] * len(ids))], local_sem=S.ls)
+        n["ls"] += _bits(hx)
 
-    after("v", g=1)
-    a = done("v", V.tensor_scalar(T.lcoli[:], T.pcol[:], 15, None, Op.bitwise_and))
-    done("v", V.tensor_scalar(T.hcoli[:], T.pcol[:], 7, None, Op.bitwise_and))
-    a = done("v", V.tensor_scalar(T.icoli[:], T.pcol[:], 3, None, Op.arith_shift_right))
+    for k in range(KS):
+        done("v", V.memset(T.kio[:, k::KS], mine[k] if k < len(mine) else -2))
     done("v", V.memset(T.ones[:], 1.0))
+    after("v", g=1)
+    done("v", V.tensor_scalar(T.ci[:, 1:2], T.ci[:, 0:1], 7, None, Op.bitwise_and))
+    done("v", V.tensor_scalar(T.ci[:, 2:3], T.ci[:, 0:1], 3, None, Op.arith_shift_right))
+    done("v", V.tensor_scalar(T.ci[:, 3:4], T.ci[:, 0:1], 3, 1, Op.arith_shift_right, Op.bitwise_and))
+    a = done("v", V.tensor_scalar(T.ci[:, 4:5], T.ci[:, 0:1], 15, None, Op.bitwise_and))
+    after("v", v=a)
+    a = done("v", V.tensor_copy(T.cf[:, 0:5], T.ci[:, 0:5]))
+    pf, hf, jf, bf, lf = [T.cf[:, q:q + 1] for q in range(5)]
+    after("v", v=a, g=2)
+    offe = done("v", V.tensor_scalar(T.offe[:], T.frow[:, 0:8:2], bf, None, Op.add))
+    a = done("v", V.tensor_scalar(T.kcol[:], hf, 16.0, jf, Op.mult, Op.add))
+    after("v", v=a, g=3)
+    done("v", V.tensor_scalar(T.mdg[:], T.krow[:], T.kcol[:], None, Op.is_gt))
+    after("v", g=4)
+    done("v", V.tensor_scalar(T.mle[:], T.hrow[:], hf, None, Op.is_ge))
+    done("v", V.tensor_scalar(T.mlt[:], T.hrow[:], hf, None, Op.is_gt))
+    kdone = done("v", V.tensor_scalar(T.k256[0:1, :], T.hrow[0:1, 0:KC], float(CAPP), None, Op.mult))
+    bdone = done("v", V.tensor_scalar(T.bigi[:], T.frow[:], pf, BIG, Op.is_equal, Op.mult))
+    if main:
+        need("v", "ldex", 16)
+    else:
+        need("v", "hex", _bits(hx))
+    ohd = done("v", V.tensor_tensor(T.oh[:], T.exsb[:].indirect(T.offe[:]), T.kio[:], Op.is_equal))
+    b = done("v", V.tensor_scalar(T.jb[:], hf, 128.0, jf, Op.mult, Op.add))
+    done("v", V.tensor_scalar(T.resetm[:], T.hrow[:, 0:KC], 0.0, None, Op.is_gt))
     if main:
         done("v", V.memset(T.land[:, ZERO:ZERO + 16], 0.0))
-    after("v", v=a)
-    done("v", V.tensor_copy(T.lcol[:], T.lcoli[:]))
-    done("v", V.tensor_copy(T.hcol[:], T.hcoli[:]))
-    done("v", V.tensor_copy(T.icol[:], T.icoli[:]))
-    a = done("v", V.tensor_copy(T.pcolf[:], T.pcol[:]))
-    after("v", v=a, g=2)
-    b = done("v", V.tensor_scalar(T.otf[:], T.frow[:, 0:NC + 1], 16.0, T.lcol[:], Op.mult, Op.add))
-    done("v", V.tensor_scalar(T.bigi[:], T.frow[:], T.pcolf[:], BIG, Op.is_equal, Op.mult))
-    a = done("v", V.tensor_scalar(T.kcol[:], T.hcoli[:], 128.0, T.icol[:], Op.mult, Op.add))
     after("v", v=b)
-    b = done("v", V.tensor_scalar(T.oti[:], T.otf[:], -8.5, 1.0 / E, Op.add, Op.mult))
-    after("v", g=5)
-    done("v", V.tensor_scalar(T.mlt[:], T.hrow[:], T.hcol[:], None, Op.is_gt))
-    done("v", V.tensor_scalar(T.mle[:], T.hrow[:], T.hcol[:], None, Op.is_ge))
-    after("v", v=b)
-    b = done("v", V.tensor_copy(T.offe[:, 0:NC + 1], T.oti[:]))
-    done("v", V.tensor_scalar(T.mdg[:], T.krow[:], T.kcol[:], None, Op.is_gt))
-    kdone = done("v", V.tensor_scalar(T.k256[0:1, :], T.kio[0:1, :], float(CAPP), None, Op.mult))
-    after("v", v=b)
-    if main:
-        need("v", "ldex", S.ldex, 16)
-    else:
-        need("v", "hex", S.hex, _bits(hx))
-    ohd = done("v", V.tensor_tensor(T.oh[:], T.exsb[:, 0:NC].indirect(T.offe[:, 0:NC + 1]), T.kio[:], Op.is_equal))
-    rsd = done("v", V.tensor_scalar(T.resetm[:], T.kio[:], 0, None, Op.is_gt))
-    done("v", V.tensor_scalar(T.jcol[:], T.frow[:, 0:NC], 16.0, T.kcol[:], Op.mult, Op.add))
-    b = done("v", V.tensor_scalar(T.mrowi[:], T.frow[:], 15, None, Op.bitwise_and))
-    for q, d in enumerate(blocks):
-        done("v", V.tensor_scalar(T.bio[:, 32 * q:32 * q + 32], T.frow[:, 0:32], 32.0 * d, None, Op.add))
-    after("v", v=b)
-    cd = done("v", V.tensor_copy(T.mrow[:], T.mrowi[:]))
+    cd = done("v", V.tensor_scalar(T.jcol[:], T.frow[:, 0:NC], 16.0, T.jb[:], Op.mult, Op.add))
 
     after("p", v=kdone)
     ps = T.psc
@@ -220,27 +207,25 @@ def rank_program(g, core, T, topo):
     after("p", v=ohd)
     PE.matmul(ps[:, 0:KC], T.mdg[:], T.oh[:], False, False)
     for d in range(1, NC):
-        PE.matmul(ps[:, E * d:KC], T.mle[:], T.oh[:, 0:KC - E * d], False, False)
-        PE.matmul(ps[:, 0:KC - E * d], T.mlt[:], T.oh[:, E * d:KC], False, False)
+        PE.matmul(ps[:, KS * d:KC], T.mle[:], T.oh[:, 0:KC - KS * d], False, False)
+        PE.matmul(ps[:, 0:KC - KS * d], T.mlt[:], T.oh[:, KS * d:KC], False, False)
     a = done("p", PE.matmul(ps[:, 0:KC], T.bigi[:], T.oh[:], False, True))
 
     after("v", p=a, v=cd)
     a = done("v", V.tensor_tensor_scan(T.rr[:], T.resetm[:], ps[:, 0:KC], 0.0, Op.mult, Op.max))
     after("v", v=a)
-    sl = T.rr[:, E - 1::E]
+    sl = T.rr[:, KS - 1::KS]
     a = done("v", V.tensor_scalar(T.hii[:], sl, -(BIG + 7.5), 1.0 / 16, Op.add, Op.mult))
     after("v", v=a)
     done("v", V.tensor_copy(T.hif[:], T.hii[:]))
     a = done("v", V.tensor_scalar(T.h16[:], T.hii[:], -16.0, -BIG, Op.mult, Op.add))
     after("v", v=a)
     a = done("v", V.tensor_tensor(T.lo[:], T.h16[:], sl, Op.add))
+    after("v", g=5)
     bds = []
     for c in range(NC):
-        if c == 1:
-            after("v", v=a)
-        done("v", V.tensor_scalar(T.bt[:, nb * c:nb * (c + 1)], T.bio[:, 0:nb], T.hif[:, c:c + 1], None, Op.is_equal))
-        if c == 0:
-            after("v", v=a)
+        done("v", V.tensor_scalar(T.bt[:, nb * c:nb * (c + 1)], T.frow[:, 0:nb], T.hif[:, c:c + 1], None, Op.is_equal))
+        after("v", v=a)
         bds.append(done("v", V.tensor_scalar(T.at[:, 128 * c:128 * (c + 1)], T.mrow[:], T.lo[:, c:c + 1],
                                              T.jcol[:, c:c + 1], Op.is_equal, Op.mult)))
     for c in range(NC):
@@ -253,52 +238,46 @@ def rank_program(g, core, T, topo):
     for q in ("v", "s"):
         after(q, v=offd)
         if main:
-            need(q, "ldx0", S.ldx0, 16)
-            need(q, "ldx1", S.ldx1, 16)
+            need(q, "ldx", 16)
         else:
-            need(q, "hx0", S.hx0, _bits(hm[seat]))
-            need(q, "hx1", S.hx1, _bits(hm[seat]))
-    for q, d in enumerate(blocks):
+            need(q, "hx", _bits(hx))
+    k = at = 0
+    for d, es in blocks:
+        w = CAPP * len(es)
+        dst = T.land[:, rank * W + CAPP * es[0]:rank * W + CAPP * es[0] + w]
         if d == rank:
-            o0 = T.land[:, rank * W:rank * W + CAPP]
-            o1 = T.land[:, rank * W + CAPP:(rank + 1) * W]
+            base, buf = rank * W, T.land
         else:
-            o0 = T.pk[:, q * W:q * W + CAPP]
-            o1 = T.pk[:, q * W + CAPP:(q + 1) * W]
-        va = done("v", V.tensor_copy(o0, T.xs[:].indirect(T.offu[:, 32 * q:32 * q + 16])))
-        sa = done("s", SC.activation(o1, T.xs[:].indirect(T.offu[:, 32 * q + 16:32 * q + 32]), Act.Copy))
+            base, buf = at, T.pk
+            at += w
+        h, f = w // 2, 16 * k
+        va = done("v", V.tensor_copy(buf[:, base:base + h], T.xs[:].indirect(T.offu[:, f:f + h // 16])))
+        sa = done("s", SC.activation(buf[:, base + h:base + w], T.xs[:].indirect(T.offu[:, f + h // 16:f + w // 16]), Act.Copy))
+        k += len(es)
         if d != rank:
             after("g", v=va, s=sa)
             rid, pid = topo.addr(T.cores[d], core)
             m = topo.mask(core, T.cores[d])
-            g.remote_dma(T.land[:, rank * W:(rank + 1) * W], T.pk[:, q * W:(q + 1) * W], S.arr, S.ls, pid, rid, m)
+            g.remote_dma(dst, T.pk[:, base:base + w], S.arr, S.ls, pid, rid, m)
             n["ls"] += _bits(m)
 
     if main:
-        done("v", V.tensor_scalar(T.ident[:], T.frow[:], T.pcolf[:], None, Op.is_equal))
-        b = done("v", V.tensor_scalar(T.pl[:], T.frow[:, 0:LW], 16.0, T.lcol[:], Op.mult, Op.add))
-        done("v", V.tensor_scalar(T.rmask[0:8 * N, :], T.frow[0:8 * N, 0:10], T.icol[0:8 * N, :], None, Op.is_gt))
+        done("v", V.tensor_scalar(T.ident[:], T.frow[:], pf, None, Op.is_equal))
+        b = done("v", V.tensor_scalar(T.pl[:], T.frow[:, 0:LW], 16.0, lf, Op.mult, Op.add))
+        done("v", V.tensor_scalar(T.rmask[0:8 * N, :], T.frow[0:8 * N, 0:10], T.cf[0:8 * N, 2:3], None, Op.is_gt))
         after("v", v=b)
         for e in range(EL):
             done("v", V.tensor_scalar(T.plb[:, e * LW:(e + 1) * LW], T.pl[:], float(e * CAPP), None, Op.add))
-        total = 0
-        exn = 0
+        total = exn = 0
         for r in range(N):
-            if r != rank:
-                mm = 0xFFFFFFFF
-                for d in T.cores:
-                    if d != T.cores[r]:
-                        mm &= topo.mask(T.cores[r], d)
-                exn += _bits(mm)
-                tm = _team(r, T, topo)
-                for i, p in enumerate(PLAN):
-                    for s in p:
-                        if (r + s) % N == rank:
-                            total += _bits(topo.mask(tm[i], core))
-        need("y", "ldexd", S.ldexd, 16)
-        need("y", "exarr", S.exarr, exn)
+            for i in range(len(PLAN)):
+                m = _bits(topo.mask(teams[r][i], core)) if r != rank else 0
+                total += m * sum((r + s) % N == rank for s, es in PLAN[i])
+                exn += m * sum((r + s) % N == rank for s in LISTS[i])
+        need("y", "ldexd", 16)
+        need("y", "exarr", exn)
         g.sync.dma_start(T.exs[0:8 * N, :], T.exall[:]).then_inc(S.ldexs, 16)
-        need("v", "ldexs", S.ldexs, 16)
+        need("v", "ldexs", 16)
         for e in range(EL):
             b = done("v", V.tensor_scalar(T.eqt[0:8 * N, 128 * e:128 * e + 128], T.exs[0:8 * N, :], EL * rank + e, None,
                                           Op.is_equal))
@@ -331,15 +310,15 @@ def rank_program(g, core, T, topo):
         b = done("v", V.tensor_scalar(T.offy[:], T.psi[:, 0:EL * LW], float(ZERO), None, Op.min))
         after("v", v=b, s=n["s"])
         after("s", v=b, s=n["s"])
-        need("v", "arr", S.arr, total)
-        need("s", "arr", S.arr, total)
+        need("v", "arr", total)
+        need("s", "arr", total)
         a = done("v", V.tensor_copy(T.yt[:, 0:CAP], T.land[:].indirect(T.offy[:, 0:LW])))
         b = done("s", SC.activation(T.yt[:, CAP:2 * CAP], T.land[:].indirect(T.offy[:, LW:2 * LW]), Act.Copy))
         after("y", v=a)
         g.sync.dma_start(T.y[:, 0:CAP], T.yt[:, 0:CAP]).then_inc(S.sty0, 16)
         after("s", s=b)
         g.scalar.dma_start(T.y[:, CAP:2 * CAP], T.yt[:, CAP:2 * CAP]).then_inc(S.sty1, 16)
-        need("g", "sty0", S.sty0, 16)
-        need("g", "sty1", S.sty1, 16)
+        need("g", "sty0", 16)
+        need("g", "sty1", 16)
     after("g", v=n["v"], s=n["s"], p=n["p"], g=n["g"])
     g.wait_ge(S.ls, n["ls"])

from concourse.bass import DstId, RemoteDMATransfer
from concourse.mybir import AluOpType as Op, AxisListType, ActivationFunctionType as Act

N, T_, EL, CAP, CAPP = 9, 1024, 2, 480, 256
E = N * EL
W = EL * CAPP
ZERO = N * W
NC = 8
KS = 8
KC = NC * KS
BIG = 8192.0
LW = CAP // 16

PLAN = [[(2, (0, 1)), (6, (0, 1)), (7, (0,))], [(1, (0, 1)), (5, (0, 1))], [(4, (0, 1)), (8, (0, 1))],
        [(3, (0, 1)), (7, (1,))]]
FEED = [None, 0, 0, 1]
LISTS = [[], [1, 5], [2, 6, 8], [3, 7, 4]]
NBMAX = 16 * 7

SCRATCH = {
    "xs": ("sbuf", [128, T_], "float32"),
    "exsb": ("sbuf", [128, NC], "int32"),
    "exall": ("dram", [N * 128, NC], "int32"),
    "exs": ("sbuf", [128, 128], "int32"),
    "land": ("sbuf", [128, N * W + 16], "float32"),
    "pk": ("sbuf", [128, 3 * W], "float32"),
    "yt": ("sbuf", [128, EL * CAP], "float32"),
    "ci": ("sbuf", [128, 8], "int32"),
    "cf": ("sbuf", [128, 8], "float32"),
    "kcol": ("sbuf", [128, 1], "float32"),
    "jb": ("sbuf", [128, 1], "float32"),
    "kio": ("sbuf", [128, KC], "int32"),
    "frow": ("sbuf", [128, 128], "bfloat16"),
    "hrow": ("sbuf", [128, 128], "bfloat16"),
    "krow": ("sbuf", [128, 128], "bfloat16"),
    "mrow": ("sbuf", [128, 128], "bfloat16"),
    "offe": ("sbuf", [128, 4], "uint16"),
    "mlt": ("sbuf", [128, 128], "bfloat16"),
    "mle": ("sbuf", [128, 128], "bfloat16"),
    "mdg": ("sbuf", [128, 128], "bfloat16"),
    "bigi": ("sbuf", [128, 128], "bfloat16"),
    "ones": ("sbuf", [128, 128], "bfloat16"),
    "k256": ("sbuf", [128, KC], "bfloat16"),
    "resetm": ("sbuf", [128, KC], "float32"),
    "oh": ("sbuf", [128, KC], "bfloat16"),
    "rr": ("sbuf", [128, KC], "float32"),
    "jcol": ("sbuf", [128, NC], "float32"),
    "hii": ("sbuf", [128, NC], "int32"),
    "hif": ("sbuf", [128, NC], "float32"),
    "h16": ("sbuf", [128, NC], "float32"),
    "lo": ("sbuf", [128, NC], "float32"),
    "at": ("sbuf", [128, NC * 128], "float16"),
    "bt": ("sbuf", [128, NC * NBMAX], "float16"),
    "offu": ("sbuf", [128, NBMAX], "uint16"),
    "ident": ("sbuf", [128, 128], "float16"),
    "pl": ("sbuf", [128, LW], "float16"),
    "plb": ("sbuf", [128, EL * LW], "float16"),
    "rmask": ("sbuf", [128, 10], "bfloat16"),
    "eqt": ("sbuf", [128, EL * 128], "float32"),
    "cnt": ("sbuf", [128, EL], "float32"),
    "prhs": ("sbuf", [128, EL * 10], "bfloat16"),
    "pst": ("sbuf", [128, EL * 10], "float32"),
    "pdf": ("sbuf", [128, EL * 10], "float32"),
    "jmp": ("sbuf", [128, EL * 10], "float32"),
    "tt": ("sbuf", [128, N * EL * LW], "float16"),
    "offy": ("sbuf", [128, EL * LW], "uint16"),
    "psc": ("psum", [128, 512], "float32"),
    "pso": ("psum", [128, 512], "float32"),
    "psp": ("psum", [128, 512], "float32"),
    "psi": ("psum", [128, 512], "float32"),
}
SEMAPHORES = ["gi", "vs", "ss", "pe", "ldex", "ldexd", "ldx", "ldexs", "sty0", "sty1", "hex", "hx", "exarr", "arr", "ls"]


def _bits(m):
    return bin(m).count("1")


def _team(rank, T, topo):
    me = T.cores[rank]
    same = [c for c in range(256) if topo.host(c) == topo.host(me) and topo.chip(c) == topo.chip(me)
            and c != me and all(topo.may_write(c, d) for d in T.cores)]
    far = [c for c in same if topo.die(c) != topo.die(me)]
    near = [c for c in same if topo.die(c) == topo.die(me)]
    return [me, far[0], near[0], far[1]]


def rank_program(g, core, T, topo):
    teams = [_team(r, T, topo) for r in range(N)]
    rank = None
    for r in range(N):
        if core in teams[r]:
            rank, seat = r, teams[r].index(core)
    if rank is None:
        return
    team = teams[rank]
    main = seat == 0
    blocks = [((rank + s) % N, es) for s, es in PLAN[seat]] + ([(rank, (0, 1))] if main else [])
    mine = [EL * d + e for d, es in blocks for e in es]
    nb = 16 * len(mine)
    S = T.sem
    n = {"v": 0, "s": 0, "p": 0, "g": 0, "ls": 0}
    eng = {"v": g.vector, "s": g.scalar, "p": g.tensor, "g": g, "y": g.sync}
    semof = {"v": S.vs, "s": S.ss, "p": S.pe, "g": S.gi}
    seen = {}

    def need(q, name, val):
        if val > 0 and seen.get((q, name), 0) < val:
            eng[q].wait_ge(semof[name] if name in semof else S[name], val)
            seen[(q, name)] = val

    def after(q, **k):
        for name, val in k.items():
            need(q, name, val)

    def done(q, ins):
        ins.then_inc(semof[q], 1)
        n[q] += 1
        return n[q]

    V, PE, SC = g.vector, g.tensor, g.scalar

    if main:
        g.sync.dma_start(T.exsb[:], T.ex[:]).then_inc(S.ldex, 16)
        g.scalar.dma_start(T.exall[rank * 128:(rank + 1) * 128, :], T.ex[:]).then_inc(S.ldexd, 16)
        g.sync.dma_start(T.xs[:], T.x[:]).then_inc(S.ldx, 16)
    hx = topo.mask(team[0], team[1]) & topo.mask(team[0], team[2]) & topo.mask(team[0], team[3])

    fl = {"allow_small_or_imprecise_dtypes": True}
    done("g", g.iota(T.ci[:, 0:1], [[0, 1]], 0, 1))
    done("g", g.iota(T.frow[:], [[1, 128]], 0, 0, **fl))
    done("g", g.iota(T.krow[:], [[1, 16], [16, 8]], 0, 0, **fl))
    done("g", g.iota(T.hrow[:], [[0, 16], [1, 8]], 0, 0, **fl))

    slot = T.exall[rank * 128:(rank + 1) * 128, :]
    if main:
        need("g", "ldexd", 16)
        ids = []
        for c in team[1:]:
            rid, pid = topo.addr(c, core)
            ids.append(DstId(rid=rid, pnc=pid))
        g.remote_dma_fused([RemoteDMATransfer(dst_ids=ids, dma_engine_mask=hx, remote_sem=S.hex, srcs=[slot],
                                              dsts=[T.exsb[:]] * len(ids))], local_sem=S.ls)
        n["ls"] += _bits(hx)
    done("g", g.iota(T.mrow[:], [[0, 8], [1, 16]], 0, 0, **fl))
    if LISTS[seat]:
        need("g", "hex", _bits(hx))
        ids, mask = [], topo.mask(core, T.cores[(rank + LISTS[seat][0]) % N])
        for s in LISTS[seat]:
            d = T.cores[(rank + s) % N]
            rid, pid = topo.addr(d, core)
            ids.append(DstId(rid=rid, pnc=pid))
            mask &= topo.mask(core, d)
        g.remote_dma_fused([RemoteDMATransfer(dst_ids=ids, dma_engine_mask=mask, remote_sem=S.exarr,
                                              srcs=[T.exsb[:]], dsts=[slot] * len(ids))], local_sem=S.ls)
        n["ls"] += _bits(mask)
    fed = [team[i] for i in range(len(team)) if FEED[i] == seat]
    if fed:
        if main:
            need("g", "ldx", 16)
        else:
            need("g", "hx", _bits(hx))
        ids = []
        for c in fed:
            rid, pid = topo.addr(c, core)
            ids.append(DstId(rid=rid, pnc=pid))
        g.remote_dma_fused([RemoteDMATransfer(dst_ids=ids, dma_engine_mask=hx, remote_sem=S.hx, srcs=[T.xs[:]],
                                              dsts=[T.xs[:]] * len(ids))], local_sem=S.ls)
        n["ls"] += _bits(hx)

    for k in range(KS):
        done("v", V.memset(T.kio[:, k::KS], mine[k] if k < len(mine) else -2))
    done("v", V.memset(T.ones[:], 1.0))
    after("v", g=1)
    done("v", V.tensor_scalar(T.ci[:, 1:2], T.ci[:, 0:1], 7, None, Op.bitwise_and))
    done("v", V.tensor_scalar(T.ci[:, 2:3], T.ci[:, 0:1], 3, None, Op.arith_shift_right))
    done("v", V.tensor_scalar(T.ci[:, 3:4], T.ci[:, 0:1], 3, 1, Op.arith_shift_right, Op.bitwise_and))
    a = done("v", V.tensor_scalar(T.ci[:, 4:5], T.ci[:, 0:1], 15, None, Op.bitwise_and))
    after("v", v=a)
    a = done("v", V.tensor_copy(T.cf[:, 0:5], T.ci[:, 0:5]))
    pf, hf, jf, bf, lf = [T.cf[:, q:q + 1] for q in range(5)]
    after("v", v=a, g=2)
    offe = done("v", V.tensor_scalar(T.offe[:], T.frow[:, 0:8:2], bf, None, Op.add))
    a = done("v", V.tensor_scalar(T.kcol[:], hf, 16.0, jf, Op.mult, Op.add))
    after("v", v=a, g=3)
    done("v", V.tensor_scalar(T.mdg[:], T.krow[:], T.kcol[:], None, Op.is_gt))
    after("v", g=4)
    done("v", V.tensor_scalar(T.mle[:], T.hrow[:], hf, None, Op.is_ge))
    done("v", V.tensor_scalar(T.mlt[:], T.hrow[:], hf, None, Op.is_gt))
    kdone = done("v", V.tensor_scalar(T.k256[0:1, :], T.hrow[0:1, 0:KC], float(CAPP), None, Op.mult))
    bdone = done("v", V.tensor_scalar(T.bigi[:], T.frow[:], pf, BIG, Op.is_equal, Op.mult))
    if main:
        need("v", "ldex", 16)
    else:
        need("v", "hex", _bits(hx))
    ohd = done("v", V.tensor_tensor(T.oh[:], T.exsb[:].indirect(T.offe[:]), T.kio[:], Op.is_equal))
    b = done("v", V.tensor_scalar(T.jb[:], hf, 128.0, jf, Op.mult, Op.add))
    done("v", V.tensor_scalar(T.resetm[:], T.hrow[:, 0:KC], 0.0, None, Op.is_gt))
    if main:
        done("v", V.memset(T.land[:, ZERO:ZERO + 16], 0.0))
    after("v", v=b)
    cd = done("v", V.tensor_scalar(T.jcol[:], T.frow[:, 0:NC], 16.0, T.jb[:], Op.mult, Op.add))

    after("p", v=kdone)
    ps = T.psc
    PE.matmul(ps[:, 0:KC], T.ones[0:1, :], T.k256[0:1, :], True, False)
    after("p", v=ohd)
    PE.matmul(ps[:, 0:KC], T.mdg[:], T.oh[:], False, False)
    for d in range(1, NC):
        PE.matmul(ps[:, KS * d:KC], T.mle[:], T.oh[:, 0:KC - KS * d], False, False)
        PE.matmul(ps[:, 0:KC - KS * d], T.mlt[:], T.oh[:, KS * d:KC], False, False)
    a = done("p", PE.matmul(ps[:, 0:KC], T.bigi[:], T.oh[:], False, True))

    after("v", p=a, v=cd)
    a = done("v", V.tensor_tensor_scan(T.rr[:], T.resetm[:], ps[:, 0:KC], 0.0, Op.mult, Op.max))
    after("v", v=a)
    sl = T.rr[:, KS - 1::KS]
    a = done("v", V.tensor_scalar(T.hii[:], sl, -(BIG + 7.5), 1.0 / 16, Op.add, Op.mult))
    after("v", v=a)
    done("v", V.tensor_copy(T.hif[:], T.hii[:]))
    a = done("v", V.tensor_scalar(T.h16[:], T.hii[:], -16.0, -BIG, Op.mult, Op.add))
    after("v", v=a)
    a = done("v", V.tensor_tensor(T.lo[:], T.h16[:], sl, Op.add))
    after("v", g=5)
    bds = []
    for c in range(NC):
        done("v", V.tensor_scalar(T.bt[:, nb * c:nb * (c + 1)], T.frow[:, 0:nb], T.hif[:, c:c + 1], None, Op.is_equal))
        after("v", v=a)
        bds.append(done("v", V.tensor_scalar(T.at[:, 128 * c:128 * (c + 1)], T.mrow[:], T.lo[:, c:c + 1],
                                             T.jcol[:, c:c + 1], Op.is_equal, Op.mult)))
    for c in range(NC):
        after("p", v=bds[c])
        ins = PE.matmul(T.pso[:, 0:nb], T.at[:, 128 * c:128 * (c + 1)], T.bt[:, nb * c:nb * (c + 1)], c == 0, c == NC - 1)
    a = done("p", ins)
    after("v", p=a)
    offd = done("v", V.tensor_copy(T.offu[:, 0:nb], T.pso[:, 0:nb]))

    for q in ("v", "s"):
        after(q, v=offd)
        if main:
            need(q, "ldx", 16)
        else:
            need(q, "hx", _bits(hx))
    k = at = 0
    for d, es in blocks:
        w = CAPP * len(es)
        dst = T.land[:, rank * W + CAPP * es[0]:rank * W + CAPP * es[0] + w]
        if d == rank:
            base, buf = rank * W, T.land
        else:
            base, buf = at, T.pk
            at += w
        h, f = w // 2, 16 * k
        va = done("v", V.tensor_copy(buf[:, base:base + h], T.xs[:].indirect(T.offu[:, f:f + h // 16])))
        sa = done("s", SC.activation(buf[:, base + h:base + w], T.xs[:].indirect(T.offu[:, f + h // 16:f + w // 16]), Act.Copy))
        k += len(es)
        if d != rank:
            after("g", v=va, s=sa)
            rid, pid = topo.addr(T.cores[d], core)
            m = topo.mask(core, T.cores[d])
            g.remote_dma(dst, T.pk[:, base:base + w], S.arr, S.ls, pid, rid, m)
            n["ls"] += _bits(m)

    if main:
        done("v", V.tensor_scalar(T.ident[:], T.frow[:], pf, None, Op.is_equal))
        b = done("v", V.tensor_scalar(T.pl[:], T.frow[:, 0:LW], 16.0, lf, Op.mult, Op.add))
        done("v", V.tensor_scalar(T.rmask[0:8 * N, :], T.frow[0:8 * N, 0:10], T.cf[0:8 * N, 2:3], None, Op.is_gt))
        after("v", v=b)
        for e in range(EL):
            done("v", V.tensor_scalar(T.plb[:, e * LW:(e + 1) * LW], T.pl[:], float(e * CAPP), None, Op.add))
        total = exn = 0
        for r in range(N):
            for i in range(len(PLAN)):
                m = _bits(topo.mask(teams[r][i], core)) if r != rank else 0
                total += m * sum((r + s) % N == rank for s, es in PLAN[i])
                exn += m * sum((r + s) % N == rank for s in LISTS[i])
        need("y", "ldexd", 16)
        need("y", "exarr", exn)
        g.sync.dma_start(T.exs[0:8 * N, :], T.exall[:]).then_inc(S.ldexs, 16)
        need("v", "ldexs", 16)
        for e in range(EL):
            b = done("v", V.tensor_scalar(T.eqt[0:8 * N, 128 * e:128 * e + 128], T.exs[0:8 * N, :], EL * rank + e, None,
                                          Op.is_equal))
        after("v", v=b)
        for e in range(EL):
            b = done("v", V.tensor_reduce(T.cnt[0:8 * N, e:e + 1], T.eqt[0:8 * N, 128 * e:128 * e + 128], AxisListType.X, Op.add))
        after("v", v=b)
        for e in range(EL):
            b = done("v", V.tensor_scalar(T.prhs[0:8 * N, 10 * e:10 * e + 10], T.rmask[0:8 * N, :], T.cnt[0:8 * N, e:e + 1],
                                          None, Op.mult))
        after("p", v=b)
        a = done("p", PE.matmul(T.psp[:, 0:EL * 10], T.ones[0:8 * N, :], T.prhs[0:8 * N, :], True, True))
        after("v", p=a)
        b = done("v", V.tensor_copy(T.pst[:], T.psp[:, 0:EL * 10]))
        after("v", v=b)
        b = done("v", V.tensor_tensor(T.pdf[:, 0:EL * 10 - 1], T.pst[:, 1:EL * 10], T.pst[:, 0:EL * 10 - 1], Op.subtract))
        after("v", v=b)
        b = done("v", V.tensor_scalar(T.jmp[:, 0:EL * 10 - 1], T.pdf[:, 0:EL * 10 - 1], -1.0, float(W), Op.mult, Op.add))
        after("v", v=b)
        PE.matmul(T.psi[:, 0:EL * LW], T.ident[:], T.plb[:], True, False)
        for r in range(1, N + 1):
            for e in range(EL):
                o = T.tt[:, (r - 1) * EL * LW + e * LW:(r - 1) * EL * LW + (e + 1) * LW]
                j = T.jmp[:, 10 * e + r - 1:10 * e + r] if r < N else BIG
                b = done("v", V.tensor_scalar(o, T.pl[:], T.pst[:, 10 * e + r:10 * e + r + 1], j, Op.is_ge, Op.mult))
            after("p", v=b)
            ins = PE.matmul(T.psi[:, 0:EL * LW], T.ident[:], T.tt[:, (r - 1) * EL * LW:r * EL * LW], False, r == N)
        a = done("p", ins)
        after("v", p=a)
        b = done("v", V.tensor_scalar(T.offy[:], T.psi[:, 0:EL * LW], float(ZERO), None, Op.min))
        after("v", v=b, s=n["s"])
        after("s", v=b, s=n["s"])
        need("v", "arr", total)
        need("s", "arr", total)
        a = done("v", V.tensor_copy(T.yt[:, 0:CAP], T.land[:].indirect(T.offy[:, 0:LW])))
        b = done("s", SC.activation(T.yt[:, CAP:2 * CAP], T.land[:].indirect(T.offy[:, LW:2 * LW]), Act.Copy))
        after("y", v=a)
        g.sync.dma_start(T.y[:, 0:CAP], T.yt[:, 0:CAP]).then_inc(S.sty0, 16)
        after("s", s=b)
        g.scalar.dma_start(T.y[:, CAP:2 * CAP], T.yt[:, CAP:2 * CAP]).then_inc(S.sty1, 16)
        need("g", "sty0", 16)
        need("g", "sty1", 16)
    after("g", v=n["v"], s=n["s"], p=n["p"], g=n["g"])
    g.wait_ge(S.ls, n["ls"])
